import numpy as np
import ml_dtypes


def mxq(x, axis, fmt="e4m3"):
    dtype, down = {"e4m3": (ml_dtypes.float8_e4m3fn, 7), "e5m2": (ml_dtypes.float8_e5m2, 14)}[fmt]
    v = np.moveaxis(np.asarray(x, np.float32).astype(ml_dtypes.bfloat16).astype(np.float64), axis, -1)
    blocks = v.reshape(v.shape[:-1] + (-1, 32))
    amax = np.abs(blocks).max(-1, keepdims=True)
    byte = np.maximum(np.where(amax > 0, np.frexp(amax)[1] - 1 + 127, 0) - down, 1)
    scale = np.exp2(byte - 127.0)
    codes = (blocks / scale).astype(np.float32).astype(dtype).astype(np.float64)
    return np.moveaxis((codes * scale).reshape(v.shape), -1, axis)


WIDE = False


def mx_kscale(k):
    if not WIDE:
        return np.ones(k)
    levels = np.array([10, -10, 5, -5, 0])
    if k % 512:
        return np.exp2(np.random.permutation(np.resize(levels, k // 32))).repeat(32)
    a = np.empty((k // 512, 16))
    for p in range(k // 512):
        a[p, :8] = np.random.permutation(np.resize(levels, 8))
        for g in range(8):
            far = levels[np.abs(levels - a[p, g]) >= 10]
            a[p, g + 8] = far[np.random.randint(len(far))]
    return np.exp2(a.ravel()).repeat(32)


def f64(x):
    return np.asarray(x).astype(np.float64)


def striped(idx):
    return np.tile(idx.reshape(-1, 16).T, (8, 1)).astype(np.uint16)


def unstriped(offs):
    return offs[:16].T.reshape(-1).astype(np.int64)


E2M1 = np.array([0.0, 0.5, 1.0, 1.5, 2.0, 3.0, 4.0, 6.0, -0.0, -0.5, -1.0, -1.5, -2.0, -3.0, -4.0, -6.0])


def pack_weight(w, fmt):
    k, n = w.shape
    w = f64(np.asarray(w, np.float32).astype(ml_dtypes.bfloat16)).reshape(k // 32, 32, n)
    amax = np.abs(w).max(1)
    if fmt == "e4m3":
        byte = np.frexp(amax)[1] - 1 + 127 - 7
    else:
        mant, ex = np.frexp(amax / 6.0)
        byte = np.where(mant > 0.5, ex, ex - 1) + 127
    byte = np.clip(np.where(amax > 0, byte, 1), 1, 254)
    scaled = (w * np.exp2(127.0 - byte)[:, None, :]).reshape(k, n).astype(np.float32)
    by_word = np.ascontiguousarray(scaled.reshape(k // 512, 128, 4, n).transpose(0, 1, 3, 2))
    if fmt == "e4m3":
        words = by_word.astype(ml_dtypes.float8_e4m3fn).view(np.uint8)
    else:
        c = by_word.astype(ml_dtypes.float4_e2m1fn).view(np.uint8) & 0xF
        words = (c[..., 0::2] | (c[..., 1::2] << 4)).reshape(k // 512, 128, 2 * n)
    return np.ascontiguousarray(words), np.ascontiguousarray(byte.astype(np.uint8).reshape(k // 512, 16, n))


def unpack_weight(words, scales, fmt):
    g, _, n = scales.shape
    words = np.ascontiguousarray(words).reshape(g, 128, n, -1)
    if fmt == "e4m3":
        vals = words.view(ml_dtypes.float8_e4m3fn).astype(np.float64)
    else:
        nib = np.empty((g, 128, n, 4), np.uint8)
        nib[..., 0::2] = words & 0xF
        nib[..., 1::2] = words >> 4
        vals = E2M1[nib]
    vals = vals * np.repeat(np.exp2(scales.astype(np.float64) - 127.0), 8, axis=1)[..., None]
    return vals.transpose(0, 1, 3, 2).reshape(g * 512, n)


def gelu(v):
    return 0.5 * v * (1.0 + np.tanh(np.sqrt(2.0 / np.pi) * (v + 0.044715 * v**3)))


def striped8(idx):
    return np.concatenate([v.reshape(-1, 16).T for v in idx]).astype(np.uint16)


def unstriped8(offs):
    return np.stack([offs[16 * g:16 * g + 16].T.reshape(-1) for g in range(8)]).astype(np.int64)


def heads(h, wgt, idx8):
    r = np.arange(h.shape[0])
    return wgt[r // 4 % 128] * h[r[:, None], idx8[r % 512 // 64]]


K, T, S, T2, P, H, N = 1024, 2048, 512, 1024, 512, 1024, 512

def setup_inputs():
    n = np.random.standard_normal
    s = mx_kscale(K)[:, None]
    u = mx_kscale(H)[:, None]
    tab_words, tab_scales = pack_weight(n((K, T)) * s, "e4m3")
    w2_words, w2_scales = pack_weight(1.5 * n((K, H)) / np.sqrt(K) / s, "e2m1")
    w4_words, w4_scales = pack_weight(0.4 * n((H, N)) / np.sqrt(H) / u, "e2m1")
    return {
        "tab_words": tab_words, "tab_scales": tab_scales,
        "offs": striped(np.random.permutation(T)[:S]),
        "w1": (1.5 * n((K, H)) / np.sqrt(K) / s).astype(np.float32),
        "w2_words": w2_words, "w2_scales": w2_scales,
        "page0": (1.5 * n((H, T2))).astype(np.float32),
        "offs2": striped(np.random.permutation(T2)[:S]),
        "wgs": np.exp(0.3 * n((128, S))).astype(np.float32),
        "offs3": striped8(np.stack([np.random.permutation(T2)[:P] for _ in range(8)])),
        "wgt": np.repeat(np.random.uniform(0.5, 2.0, (8, P)), 16, axis=0).astype(np.float32),
        "gain": (np.exp(0.3 * n(H)) * u[:, 0]).astype(np.float32),
        "w3": (0.4 * n((H, N)) / np.sqrt(H) / u).astype(np.float32),
        "w4_words": w4_words, "w4_scales": w4_scales,
        "mix": np.exp(0.5 * n(N)).astype(np.float32),
    }

def reference(tab_words, tab_scales, offs, w1, w2_words, w2_scales, page0, offs2, wgs, offs3, wgt, gain, w3, w4_words, w4_scales, mix):
    v = unpack_weight(tab_words, tab_scales, "e4m3")[:, unstriped(offs)]
    w2 = unpack_weight(w2_words, w2_scales, "e2m1")
    w4 = unpack_weight(w4_words, w4_scales, "e2m1")
    a = mxq(f64(w1), 0, "e4m3").T @ v
    b = w2.T @ v
    h = np.sqrt(np.square(a) + np.square(b) + 1.0)
    page = f64(page0).copy()
    page[:, unstriped(offs2)] = np.tile(f64(wgs), (H // 128, 1)) * h
    x = heads(page, f64(wgt), unstriped8(offs3))
    xq = mxq(f64(gain)[:, None] * x, 0, "e4m3")
    y1 = mxq(f64(w3), 0, "e4m3").T @ xq
    y2 = w4.T @ xq
    return f64(mix)[:, None] * y1 + y2

@@ -1,0 +1,309 @@
+from contextlib import ExitStack
+
+import concourse.mybir as mybir
+from concourse.masks import make_identity
+
+K, T, S, T2, M, H, N = 1024, 2048, 512, 1024, 512, 1024, 512
+FLOPS = 2 * (2 * K * H * S + 2 * H * N * M)
+
+F32 = mybir.dt.float32
+BF16 = mybir.dt.bfloat16
+I32 = mybir.dt.int32
+U32 = mybir.dt.uint32
+U16 = mybir.dt.uint16
+U8 = mybir.dt.uint8
+FP8X4 = mybir.dt.float8_e4m3fn_x4
+FP4X4 = mybir.dt.float4_e2m1fn_x4
+MULT = mybir.AluOpType.mult
+ADD = mybir.AluOpType.add
+ACT = mybir.ActivationFunctionType
+
+P = 128
+PACK = 4
+KP = P * PACK
+LIST = 16
+QUADS = 4
+
+
+def tile_list_tyre_wear_wall_kernel(
+    tc, tab_words, tab_scales, offs, w1, w2_words, w2_scales, page0, offs2, wgs, offs3, wgt, gain, w3,
+    w4_words, w4_scales, mix, out,
+):
+    nc = tc.nc
+    with ExitStack() as ctx:
+        lists = ctx.enter_context(tc.tile_pool(name="lists", bufs=1))
+        keep = ctx.enter_context(tc.tile_pool(name="keep", bufs=1))
+        psum = ctx.enter_context(tc.psum_pool(name="psum", bufs=1))
+
+        def sb(shape, dtype, name, tag=None):
+            return keep.tile(shape, dtype, name=name, tag=tag or name, align_bytes=64)
+
+        def bank(index, name):
+            return psum.tile([P, KP], F32, name=name, tag="bank%d" % index)
+
+        def load_scale_rows(queue, tile, scales):
+            for q in range(QUADS):
+                rows = scales[:, 4 * q : 4 * q + 4, :].rearrange("a r c -> r a c")
+                queue.dma_start(out=tile[32 * q : 32 * q + 4, :, :].bitcast(I32), in_=rows.bitcast(I32))
+
+        def load_rows(rows, name, tag):
+            raw = sb([P, PACK, rows.shape[1]], F32, name, tag)
+            nc.sync.dma_start(out=raw[:], in_=rows.rearrange("(p i) c -> p i c", i=PACK))
+            return raw
+
+        def round_and_interleave(planes, name, tag):
+            width = planes.shape[2]
+            grouped = sb([P, width, PACK], BF16, name, tag)
+            nc.scalar.copy(
+                out=grouped[:].rearrange("p (c u) i -> p c i u", u=4),
+                in_=planes.rearrange("p i (c u) -> p c i u", u=4),
+            )
+            return grouped
+
+        def quantize(grouped, name):
+            width = grouped.shape[1]
+            codes = sb([P, width], U32, name + "_codes")
+            scales = sb([P, width], U8, name + "_scales")
+            nc.vector.quantize_mx(
+                out=codes[:].bitcast(FP8X4), scales=scales[:], in_=grouped[:].rearrange("p c i -> p (c i)")
+            )
+            return codes, scales
+
+        tab_s = sb([P, 2, T], U8, "tab_s")
+        nc.vector.memset(tab_s[:].bitcast(I32), 0)
+        w2_s = sb([P, 2, H], U8, "w2_s")
+        w4_s = sb([P, 2, N], U8, "w4_s")
+        nc.gpsimd.memset(w2_s[:].bitcast(I32), 0)
+        nc.gpsimd.memset(w4_s[:].bitcast(I32), 0)
+        one = sb([P, 1], F32, "one")
+        nc.gpsimd.memset(one[:], 1.0)
+
+        idx = lists.tile([P, S // LIST], U16, name="idx")
+        idx2 = lists.tile([P, S // LIST], U16, name="idx2")
+        idx3 = lists.tile([P, M // LIST], U16, name="idx3")
+        page_rows = page0.rearrange("(b p i) t -> b i p t", b=2, i=PACK)
+        wgs_rows = wgs.rearrange("(q i) j -> q i j", i=PACK)
+        w1_raw, w2_w, tab_w, pages, wgs_d = {}, {}, {}, {}, {}
+
+        def load_w1(b, a):
+            w1_raw[b, a] = load_rows(
+                w1[KP * a : KP * (a + 1), KP * b : KP * (b + 1)], "w1_raw%d%d" % (b, a), "raw%d%d" % (b, a)
+            )
+
+        def load_w2(b):
+            w2_w[b] = sb([P, 2, 2 * KP], U8, "w2_w%d" % b)
+            src = w2_words[:, :, 2 * KP * b : 2 * KP * (b + 1)].rearrange("a p c -> p a c")
+            nc.sync.dma_start(out=w2_w[b][:].bitcast(I32), in_=src.bitcast(I32))
+
+        def load_tab(a):
+            tab_w[a] = sb([P, T], I32, "tab_w%d" % a)
+            nc.sync.dma_start(out=tab_w[a][:], in_=tab_words[a].rearrange("p t i -> p (t i)").bitcast(I32))
+
+        def load_page(b, i):
+            pages[b, i] = sb([P, T2], F32, "page%d%d" % (b, i))
+            nc.sync.dma_start(out=pages[b, i][:], in_=page_rows[b, i])
+
+        def load_wgs(pair):
+            wgs_d[pair] = sb([P, 2, S], F32, "wgs%d" % pair)
+            for q in range(QUADS):
+                nc.sync.dma_start(
+                    out=wgs_d[pair][32 * q : 32 * (q + 1), :, :], in_=wgs_rows[:, 2 * pair : 2 * pair + 2, :]
+                )
+
+        nc.sync.dma_start(idx[:], offs)
+        load_w1(0, 0)
+        load_scale_rows(nc.sync, tab_s, tab_scales)
+        load_w1(0, 1)
+        load_w2(0)
+        load_tab(0)
+        load_tab(1)
+        nc.sync.dma_start(idx2[:], offs2)
+        wgt_t = sb([P, M], F32, "wgt_t")
+        nc.sync.dma_start(out=wgt_t[:], in_=wgt)
+        load_page(0, 0)
+        load_wgs(0)
+        load_page(0, 1)
+        nc.sync.dma_start(idx3[:], offs3)
+        load_w1(1, 0)
+        load_w1(1, 1)
+        load_w2(1)
+        load_wgs(1)
+        load_page(0, 2)
+        load_page(0, 3)
+        for i in range(PACK):
+            load_page(1, i)
+        w4_w = sb([P, 2, 2 * N], U8, "w4_w")
+        nc.sync.dma_start(out=w4_w[:].bitcast(I32), in_=w4_words.rearrange("a p c -> p a c").bitcast(I32))
+
+        load_scale_rows(nc.gpsimd, w2_s, w2_scales)
+        gain_t = sb([P, 2, PACK], F32, "gain_t")
+        nc.gpsimd.dma_start(out=gain_t[:], in_=gain.rearrange("(b p i) -> p b i", b=2, i=PACK))
+        ident = sb([P, P], F32, "ident")
+        make_identity(nc, ident[:])
+        load_scale_rows(nc.gpsimd, w4_s, w4_scales)
+        mix_t = sb([P, N // P], F32, "mix_t")
+        with nc.allow_non_contiguous_dma(reason="one value of mix for each partition and output tile"):
+            nc.gpsimd.dma_start(out=mix_t[:], in_=mix.rearrange("(t p) -> p t", p=P))
+
+        w1_q = {}
+        for a in range(2):
+            w1_q[0, a] = quantize(round_and_interleave(w1_raw[0, a][:], "w1_bf0%d" % a, "bf%d" % a), "w1_q0%d" % a)
+
+        v_w, v_s = {}, {}
+        for a in range(2):
+            v_s[a] = sb([P, S], U8, "v_s%d" % a)
+            nc.vector.tensor_copy(v_s[a][:], tab_s[:, a, :].indirect(idx[:]))
+        v_w[0] = sb([P, S], U32, "v_w0")
+        nc.vector.tensor_copy(v_w[0][:], tab_w[0][:].bitcast(U32).indirect(idx[:]))
+        v_w[1] = sb([P, S], U32, "v_w1")
+        half = S // 2
+        for c in range(2):
+            nc.vector.tensor_copy(
+                v_w[1][:, half * c : half * (c + 1)],
+                tab_w[1][:].bitcast(U32).indirect(idx[:, half * c // LIST : half * (c + 1) // LIST]),
+            )
+
+        w3_raw = [load_rows(w3[KP * a : KP * (a + 1), :], "w3_raw%d" % a, "raw0%d" % a) for a in range(2)]
+
+        JT = S // P
+
+        def stage1(b):
+            h = sb([P, PACK, S], F32, "h%d" % b)
+
+            def mx_pass(acc, jt, a, codes, scales):
+                cols = slice(P * jt, P * (jt + 1))
+                nc.tensor.matmul_mx(
+                    out=acc[:], lhsT=v_w[a][:, cols].bitcast(FP8X4), lhsT_scale=v_s[a][:, cols],
+                    rhs=codes, rhs_scale=scales, start=(a == 0), stop=(a == 1),
+                )
+
+            def pass_w1(acc, jt, a):
+                mx_pass(acc, jt, a, w1_q[b, a][0][:].bitcast(FP8X4), w1_q[b, a][1][:])
+
+            def pass_w2(acc, jt, a):
+                mx_pass(acc, jt, a, w2_w[b][:, a, :].bitcast(FP4X4), w2_s[:, a, KP * b : KP * (b + 1)])
+
+            def square(acc, name, tag):
+                sq = sb([P, PACK, P], F32, name, tag)
+                nc.scalar.activation(sq[:], acc[:].rearrange("p (q i) -> p i q", i=PACK), ACT.Square)
+                return sq
+
+            acc_a = [bank(jt, "acc_a%d%d" % (b, jt)) for jt in range(JT)]
+            for jt in range(JT):
+                pass_w1(acc_a[jt], jt, 0)
+            for jt in range(JT):
+                acc_b = bank(4 + jt % 2, "acc_b%d%d" % (b, jt))
+                pass_w2(acc_b, jt, 0)
+                pass_w2(acc_b, jt, 1)
+                pass_w1(acc_a[jt], jt, 1)
+                sq_b = square(acc_b, "sq_b%d%d" % (b, jt), "sq_b%d" % jt)
+                sq_a = square(acc_a[jt], "sq_a%d%d" % (b, jt), "sq_a%d" % jt)
+                total = bank(6 + jt % 2, "total%d%d" % (b, jt))
+                for i in range(PACK):
+                    cols = slice(P * i, P * (i + 1))
+                    nc.tensor.matmul(total[:, cols], sq_b[:, i, :], ident[:], start=True, stop=False, is_transpose=True)
+                    nc.tensor.matmul(total[:, cols], sq_a[:, i, :], ident[:], start=False, stop=True, is_transpose=True)
+                nc.scalar.activation(
+                    h[:, :, P * jt : P * (jt + 1)], total[:].rearrange("p (i j) -> p i j", i=PACK), ACT.Sqrt,
+                    bias=one[:],
+                )
+            return h
+
+        def scatter(b, i, h, lo, hi):
+            nc.vector.tensor_tensor(
+                pages[b, i][:].indirect(idx2[:, lo // LIST : hi // LIST]),
+                h[:, i, lo:hi], wgs_d[i // 2][:, i % 2, lo:hi], MULT,
+            )
+
+        def weights(b):
+            wg = sb([P, PACK, M], F32, "wg%d" % b)
+            for i in range(PACK):
+                nc.scalar.activation(wg[:, i, :], wgt_t[:], ACT.Copy, scale=gain_t[:, b, i : i + 1])
+            return wg
+
+        def gather(dst, b, i, wg, lo, hi):
+            nc.vector.tensor_tensor(
+                dst, pages[b, i][:].indirect(idx3[:, lo // LIST : hi // LIST]), wg[:, i, lo:hi], MULT
+            )
+
+        h0 = stage1(0)
+        for lo, hi in ((0, 128), (128, 256), (256, 512)):
+            scatter(0, 0, h0, lo, hi)
+            scatter(0, 1, h0, lo, hi)
+        w1_q[1, 0] = quantize(round_and_interleave(w1_raw[1, 0][:], "w1_bf10", "bf0"), "w1_q10")
+        w1_q[1, 1] = quantize(round_and_interleave(w1_raw[1, 1][:], "w1_bf11", "x0"), "w1_q11")
+        wg0 = weights(0)
+        scatter(0, 2, h0, 0, S)
+        scatter(0, 3, h0, 0, S)
+        h1 = stage1(1)
+        wg1 = weights(1)
+        x0 = sb([P, PACK, M], F32, "x0", "x0")
+        for i in range(PACK):
+            gather(x0[:, i, :], 0, i, wg0, 0, M)
+        for i in range(PACK):
+            scatter(1, i, h1, 0, S)
+
+        w3_q = [
+            quantize(round_and_interleave(w3_raw[0][:], "w3_bf0", "sq_a3"), "w3_q0"),
+            quantize(round_and_interleave(w3_raw[1][:], "w3_bf1", "sq_b3"), "w3_q1"),
+        ]
+        x0_q = quantize(round_and_interleave(x0[:], "x0_bf", "sq_a3"), "x0_q")
+
+        NT = N // P
+        MQ = M // P
+
+        def stage2_pass(acc1, acc2, a, codes, scales):
+            for t in range(NT):
+                cols = slice(P * t, P * (t + 1))
+                nc.tensor.matmul_mx(
+                    out=acc1[:, cols], lhsT=w3_q[a][0][:, cols].bitcast(FP8X4), lhsT_scale=w3_q[a][1][:, cols],
+                    rhs=codes, rhs_scale=scales, start=(a == 0 and t == 0), stop=(a == 1 and t == NT - 1),
+                )
+            for t in range(NT):
+                cols = slice(P * t, P * (t + 1))
+                nc.tensor.matmul_mx(
+                    out=acc2[:, cols], lhsT=w4_w[:, a, 2 * P * t : 2 * P * (t + 1)].bitcast(FP4X4),
+                    lhsT_scale=w4_s[:, a, cols],
+                    rhs=codes, rhs_scale=scales, start=(a == 0 and t == 0), stop=(a == 1 and t == NT - 1),
+                )
+
+        y1 = [bank(2 * q, "y1_%d" % q) for q in range(MQ)]
+        y2 = [bank(2 * q + 1, "y2_%d" % q) for q in range(MQ)]
+        for q in range(MQ):
+            cols = slice(P * q, P * (q + 1))
+            stage2_pass(y1[q], y2[q], 0, x0_q[0][:, cols].bitcast(FP8X4), x0_q[1][:, cols])
+
+        out_rows = out.rearrange("(t p) m -> p t m", p=P)
+        x1_first = sb([P, 2, PACK, P], F32, "x1_first", "sq_a3")
+
+        def gather_quarter(q):
+            if q < 2:
+                x1 = x1_first[:, q, :, :]
+            else:
+                x1 = sb([P, PACK, P], F32, "x1_%d" % q, "x1_bf%d" % (q - 2))[:]
+            for i in range(PACK):
+                gather(x1[:, i, :], 1, i, wg1, P * q, P * (q + 1))
+            return round_and_interleave(x1, "x1_bf%d" % q, "x1_bf%d" % q)
+
+        def multiply_quarter(q, grouped):
+            codes, scales = quantize(grouped, "x1_q%d" % q)
+            stage2_pass(y1[q], y2[q], 1, codes[:].bitcast(FP8X4), scales[:])
+
+        def finish_quarter(q):
+            mixed = sb([P, NT, P], F32, "mixed%d" % q)
+            for t in range(NT):
+                nc.scalar.activation(
+                    mixed[:, t, :], y1[q][:, P * t : P * (t + 1)], ACT.Copy, scale=mix_t[:, t : t + 1]
+                )
+            result = sb([P, NT, P], F32, "result%d" % q)
+            nc.vector.tensor_tensor(result[:], y2[q][:].rearrange("p (t m) -> p t m", t=NT), mixed[:], ADD)
+            nc.sync.dma_start(out=out_rows[:, :, P * q : P * (q + 1)], in_=result[:])
+
+        grouped = {0: gather_quarter(0)}
+        for q in range(MQ):
+            if q + 1 < MQ:
+                grouped[q + 1] = gather_quarter(q + 1)
+            multiply_quarter(q, grouped[q])
+            if q > 0:
+                finish_quarter(q - 1)
+        finish_quarter(MQ - 1)

@@ -22,7 +22,7 @@ P = 128
 PACK = 4
 KP = P * PACK
 LIST = 16
-QUADS = 4
+QUAD_ORDER = (0, 2, 1, 3)
 
 
 def tile_list_tyre_wear_wall_kernel(
@@ -42,7 +42,7 @@ def tile_list_tyre_wear_wall_kernel(
             return psum.tile([P, KP], F32, name=name, tag="bank%d" % index)
 
         def load_scale_rows(queue, tile, scales):
-            for q in range(QUADS):
+            for q in QUAD_ORDER:
                 rows = scales[:, 4 * q : 4 * q + 4, :].rearrange("a r c -> r a c")
                 queue.dma_start(out=tile[32 * q : 32 * q + 4, :, :].bitcast(I32), in_=rows.bitcast(I32))
 
@@ -51,18 +51,18 @@ def tile_list_tyre_wear_wall_kernel(
             nc.sync.dma_start(out=raw[:], in_=rows.rearrange("(p i) c -> p i c", i=PACK))
             return raw
 
-        def round_and_interleave(planes, name, tag):
+        def round_and_interleave(planes, name, tag, copy=nc.scalar.copy):
             width = planes.shape[2]
             grouped = sb([P, width, PACK], BF16, name, tag)
-            nc.scalar.copy(
+            copy(
                 out=grouped[:].rearrange("p (c u) i -> p c i u", u=4),
                 in_=planes.rearrange("p i (c u) -> p c i u", u=4),
             )
             return grouped
 
-        def quantize(grouped, name):
+        def quantize(grouped, name, tag=None):
             width = grouped.shape[1]
-            codes = sb([P, width], U32, name + "_codes")
+            codes = sb([P, width], U32, name + "_codes", tag)
             scales = sb([P, width], U8, name + "_scales")
             nc.vector.quantize_mx(
                 out=codes[:].bitcast(FP8X4), scales=scales[:], in_=grouped[:].rearrange("p c i -> p (c i)")
@@ -73,10 +73,12 @@ def tile_list_tyre_wear_wall_kernel(
         nc.vector.memset(tab_s[:].bitcast(I32), 0)
         w2_s = sb([P, 2, H], U8, "w2_s")
         w4_s = sb([P, 2, N], U8, "w4_s")
-        nc.gpsimd.memset(w2_s[:].bitcast(I32), 0)
-        nc.gpsimd.memset(w4_s[:].bitcast(I32), 0)
         one = sb([P, 1], F32, "one")
         nc.gpsimd.memset(one[:], 1.0)
+        warm = sb([P, 1], F32, "warm")
+        nc.scalar.activation(warm[:], one[:], ACT.Sqrt, bias=one[:])
+        ident = sb([P, P], F32, "ident")
+        make_identity(nc, ident[:])
 
         idx = lists.tile([P, S // LIST], U16, name="idx")
         idx2 = lists.tile([P, S // LIST], U16, name="idx2")
@@ -85,10 +87,9 @@ def tile_list_tyre_wear_wall_kernel(
         wgs_rows = wgs.rearrange("(q i) j -> q i j", i=PACK)
         w1_raw, w2_w, tab_w, pages, wgs_d = {}, {}, {}, {}, {}
 
-        def load_w1(b, a):
-            w1_raw[b, a] = load_rows(
-                w1[KP * a : KP * (a + 1), KP * b : KP * (b + 1)], "w1_raw%d%d" % (b, a), "raw%d%d" % (b, a)
-            )
+        def load_w1(b, a, lo, hi):
+            name = "w1_raw%d%d_%d" % (b, a, lo)
+            w1_raw[b, a, lo] = load_rows(w1[KP * a : KP * (a + 1), KP * b + lo : KP * b + hi], name, name)
 
         def load_w2(b):
             w2_w[b] = sb([P, 2, 2 * KP], U8, "w2_w%d" % b)
@@ -105,27 +106,32 @@ def tile_list_tyre_wear_wall_kernel(
 
         def load_wgs(pair):
             wgs_d[pair] = sb([P, 2, S], F32, "wgs%d" % pair)
-            for q in range(QUADS):
+            for q in QUAD_ORDER:
                 nc.sync.dma_start(
                     out=wgs_d[pair][32 * q : 32 * (q + 1), :, :], in_=wgs_rows[:, 2 * pair : 2 * pair + 2, :]
                 )
 
+        half = KP // 2
         nc.sync.dma_start(idx[:], offs)
-        load_w1(0, 0)
-        load_scale_rows(nc.sync, tab_s, tab_scales)
-        load_w1(0, 1)
-        load_w2(0)
+        load_scale_rows(nc.sync, w2_s, w2_scales)
         load_tab(0)
+        load_scale_rows(nc.sync, tab_s, tab_scales)
+        load_w2(0)
         load_tab(1)
+        for a in range(2):
+            load_w1(0, a, 0, half)
+            load_w1(0, a, half, KP)
         nc.sync.dma_start(idx2[:], offs2)
-        wgt_t = sb([P, M], F32, "wgt_t")
-        nc.sync.dma_start(out=wgt_t[:], in_=wgt)
         load_page(0, 0)
         load_wgs(0)
         load_page(0, 1)
+        wgt_t = sb([P, M], F32, "wgt_t")
+        nc.sync.dma_start(out=wgt_t[:], in_=wgt)
+        gain_t = sb([P, 2, PACK], F32, "gain_t")
+        nc.sync.dma_start(out=gain_t[:], in_=gain.rearrange("(b p i) -> p b i", b=2, i=PACK))
         nc.sync.dma_start(idx3[:], offs3)
-        load_w1(1, 0)
-        load_w1(1, 1)
+        load_w1(1, 0, 0, KP)
+        load_w1(1, 1, 0, KP)
         load_w2(1)
         load_wgs(1)
         load_page(0, 2)
@@ -134,85 +140,103 @@ def tile_list_tyre_wear_wall_kernel(
             load_page(1, i)
         w4_w = sb([P, 2, 2 * N], U8, "w4_w")
         nc.sync.dma_start(out=w4_w[:].bitcast(I32), in_=w4_words.rearrange("a p c -> p a c").bitcast(I32))
-
-        load_scale_rows(nc.gpsimd, w2_s, w2_scales)
-        gain_t = sb([P, 2, PACK], F32, "gain_t")
-        nc.gpsimd.dma_start(out=gain_t[:], in_=gain.rearrange("(b p i) -> p b i", b=2, i=PACK))
-        ident = sb([P, P], F32, "ident")
-        make_identity(nc, ident[:])
-        load_scale_rows(nc.gpsimd, w4_s, w4_scales)
+        load_scale_rows(nc.sync, w4_s, w4_scales)
         mix_t = sb([P, N // P], F32, "mix_t")
         with nc.allow_non_contiguous_dma(reason="one value of mix for each partition and output tile"):
-            nc.gpsimd.dma_start(out=mix_t[:], in_=mix.rearrange("(t p) -> p t", p=P))
+            nc.sync.dma_start(out=mix_t[:], in_=mix.rearrange("(t p) -> p t", p=P))
+        w3_raw = [load_rows(w3[KP * a : KP * (a + 1), :], "w3_raw%d" % a, "w3_raw%d" % a) for a in range(2)]
 
         w1_q = {}
-        for a in range(2):
-            w1_q[0, a] = quantize(round_and_interleave(w1_raw[0, a][:], "w1_bf0%d" % a, "bf%d" % a), "w1_q0%d" % a)
+
+        def quantize_w1(b, a, lo, tag, copy, codes_tag=None):
+            name = "w1_%d%d_%d" % (b, a, lo)
+            codes, scales = quantize(round_and_interleave(w1_raw[b, a, lo][:], name + "_bf", tag, copy), name, codes_tag)
+            w1_q.setdefault((b, a), []).append((lo, codes, scales))
 
         v_w, v_s = {}, {}
+
+        def gather_words(a):
+            v_w[a] = sb([P, S], U32, "v_w%d" % a)
+            nc.vector.tensor_copy(v_w[a][:], tab_w[a][:].bitcast(U32).indirect(idx[:]))
+
+        gather_words(0)
         for a in range(2):
             v_s[a] = sb([P, S], U8, "v_s%d" % a)
             nc.vector.tensor_copy(v_s[a][:], tab_s[:, a, :].indirect(idx[:]))
-        v_w[0] = sb([P, S], U32, "v_w0")
-        nc.vector.tensor_copy(v_w[0][:], tab_w[0][:].bitcast(U32).indirect(idx[:]))
-        v_w[1] = sb([P, S], U32, "v_w1")
-        half = S // 2
-        for c in range(2):
-            nc.vector.tensor_copy(
-                v_w[1][:, half * c : half * (c + 1)],
-                tab_w[1][:].bitcast(U32).indirect(idx[:, half * c // LIST : half * (c + 1) // LIST]),
-            )
-
-        w3_raw = [load_rows(w3[KP * a : KP * (a + 1), :], "w3_raw%d" % a, "raw0%d" % a) for a in range(2)]
+        gather_words(1)
+        for a in range(2):
+            quantize_w1(0, a, 0, "bf0", nc.vector.tensor_copy)
+            quantize_w1(0, a, half, "bf1", nc.vector.tensor_copy)
 
         JT = S // P
 
         def stage1(b):
-            h = sb([P, PACK, S], F32, "h%d" % b)
+            h = sb([P, 2, S], F32, "h%d" % b)
 
-            def mx_pass(acc, jt, a, codes, scales):
+            def mx_pass(acc, jt, a, codes, scales, start, stop):
                 cols = slice(P * jt, P * (jt + 1))
                 nc.tensor.matmul_mx(
-                    out=acc[:], lhsT=v_w[a][:, cols].bitcast(FP8X4), lhsT_scale=v_s[a][:, cols],
-                    rhs=codes, rhs_scale=scales, start=(a == 0), stop=(a == 1),
+                    out=acc, lhsT=v_w[a][:, cols].bitcast(FP8X4), lhsT_scale=v_s[a][:, cols],
+                    rhs=codes, rhs_scale=scales, start=start, stop=stop,
                 )
 
             def pass_w1(acc, jt, a):
-                mx_pass(acc, jt, a, w1_q[b, a][0][:].bitcast(FP8X4), w1_q[b, a][1][:])
+                for lo, codes, scales in w1_q[b, a]:
+                    hi = lo + codes.shape[1]
+                    mx_pass(acc[:, lo:hi], jt, a, codes[:].bitcast(FP8X4), scales[:], a == 0 and lo == 0, a == 1 and hi == KP)
 
             def pass_w2(acc, jt, a):
-                mx_pass(acc, jt, a, w2_w[b][:, a, :].bitcast(FP4X4), w2_s[:, a, KP * b : KP * (b + 1)])
+                mx_pass(acc[:], jt, a, w2_w[b][:, a, :].bitcast(FP4X4), w2_s[:, a, KP * b : KP * (b + 1)], a == 0, a == 1)
 
-            def square(acc, name, tag):
-                sq = sb([P, PACK, P], F32, name, tag)
-                nc.scalar.activation(sq[:], acc[:].rearrange("p (q i) -> p i q", i=PACK), ACT.Square)
-                return sq
+            def square(sq, acc, lo, hi):
+                planes = acc[:].rearrange("p (q i) -> p i q", i=PACK)
+                nc.scalar.activation(sq[:, lo:hi, :], planes[:, lo:hi, :], ACT.Square)
 
-            acc_a = [bank(jt, "acc_a%d%d" % (b, jt)) for jt in range(JT)]
+            def turn(total, slot, sq, start, stop):
+                nc.tensor.matmul(total[:, P * slot : P * (slot + 1)], sq, ident[:], start=start, stop=stop, is_transpose=True)
+
+            def add_turned(total, slot, jt, i):
+                turn(total, slot, sq_b[jt][:, i, :], True, False)
+                turn(total, slot, sq_a[jt][:, i, :], False, True)
+
+            sq_a, sq_b = {}, {}
             for jt in range(JT):
-                pass_w1(acc_a[jt], jt, 0)
-            for jt in range(JT):
-                acc_b = bank(4 + jt % 2, "acc_b%d%d" % (b, jt))
+                acc_a = bank(jt % 2 if b == 0 else jt, "acc_a%d%d" % (b, jt))
+                acc_b = bank(4 + jt, "acc_b%d%d" % (b, jt))
+                sq_a[jt] = sb([P, PACK, P], F32, "sq_a%d%d" % (b, jt), "sq_a%d" % jt)
+                sq_b[jt] = sb([P, PACK, P], F32, "sq_b%d%d" % (b, jt), "sq_b%d" % jt)
                 pass_w2(acc_b, jt, 0)
+                pass_w1(acc_a, jt, 0)
                 pass_w2(acc_b, jt, 1)
-                pass_w1(acc_a[jt], jt, 1)
-                sq_b = square(acc_b, "sq_b%d%d" % (b, jt), "sq_b%d" % jt)
-                sq_a = square(acc_a[jt], "sq_a%d%d" % (b, jt), "sq_a%d" % jt)
-                total = bank(6 + jt % 2, "total%d%d" % (b, jt))
-                for i in range(PACK):
-                    cols = slice(P * i, P * (i + 1))
-                    nc.tensor.matmul(total[:, cols], sq_b[:, i, :], ident[:], start=True, stop=False, is_transpose=True)
-                    nc.tensor.matmul(total[:, cols], sq_a[:, i, :], ident[:], start=False, stop=True, is_transpose=True)
+                pass_w1(acc_a, jt, 1)
+                square(sq_b[jt], acc_b, 0, PACK)
+                square(sq_a[jt], acc_a, 0, 2)
+                total = bank(4 + jt, "total%d%d" % (b, jt))
+                turn(total, 0, sq_b[jt][:, 0, :], True, False)
+                turn(total, 1, sq_b[jt][:, 1, :], False, False)
+                turn(total, 0, sq_a[jt][:, 0, :], False, False)
+                turn(total, 1, sq_a[jt][:, 1, :], False, True)
                 nc.scalar.activation(
-                    h[:, :, P * jt : P * (jt + 1)], total[:].rearrange("p (i j) -> p i j", i=PACK), ACT.Sqrt,
-                    bias=one[:],
+                    h[:, :, P * jt : P * (jt + 1)], total[:, 0 : 2 * P].rearrange("p (i j) -> p i j", i=2),
+                    ACT.Sqrt, bias=one[:],
                 )
+                square(sq_a[jt], acc_a, 2, PACK)
+            late = {}
+            for i in range(2, PACK):
+                late[i] = bank(i, "late%d%d" % (b, i))
+                for jt in range(JT):
+                    add_turned(late[i], jt, jt, i)
+            return h, late
+
+        def root(total, name, tag):
+            h = sb([P, S], F32, name, tag)
+            nc.scalar.activation(h[:], total[:], ACT.Sqrt, bias=one[:])
             return h
 
         def scatter(b, i, h, lo, hi):
             nc.vector.tensor_tensor(
                 pages[b, i][:].indirect(idx2[:, lo // LIST : hi // LIST]),
-                h[:, i, lo:hi], wgs_d[i // 2][:, i % 2, lo:hi], MULT,
+                h[:, lo:hi], wgs_d[i // 2][:, i % 2, lo:hi], MULT,
             )
 
         def weights(b):
@@ -226,28 +250,34 @@ def tile_list_tyre_wear_wall_kernel(
                 dst, pages[b, i][:].indirect(idx3[:, lo // LIST : hi // LIST]), wg[:, i, lo:hi], MULT
             )
 
-        h0 = stage1(0)
-        for lo, hi in ((0, 128), (128, 256), (256, 512)):
-            scatter(0, 0, h0, lo, hi)
-            scatter(0, 1, h0, lo, hi)
-        w1_q[1, 0] = quantize(round_and_interleave(w1_raw[1, 0][:], "w1_bf10", "bf0"), "w1_q10")
-        w1_q[1, 1] = quantize(round_and_interleave(w1_raw[1, 1][:], "w1_bf11", "x0"), "w1_q11")
+        h0, late0 = stage1(0)
+        h02 = root(late0[2], "h02", "h02")
+        h03 = root(late0[3], "h03", "h03")
+        for lo, hi in ((0, 128), (128, 256), (256, 384), (384, 512)):
+            scatter(0, 0, h0[:, 0, :], lo, hi)
+            scatter(0, 1, h0[:, 1, :], lo, hi)
+        quantize_w1(1, 0, 0, "bf0", nc.scalar.copy)
+        scatter(0, 2, h02[:], 0, S)
+        quantize_w1(1, 1, 0, "x0", nc.scalar.copy, "h02")
         wg0 = weights(0)
-        scatter(0, 2, h0, 0, S)
-        scatter(0, 3, h0, 0, S)
-        h1 = stage1(1)
+        scatter(0, 3, h03[:], 0, S)
+        h1, late1 = stage1(1)
+        h12 = root(late1[2], "h12", "h12")
         wg1 = weights(1)
         x0 = sb([P, PACK, M], F32, "x0", "x0")
         for i in range(PACK):
             gather(x0[:, i, :], 0, i, wg0, 0, M)
-        for i in range(PACK):
-            scatter(1, i, h1, 0, S)
+        scatter(1, 0, h1[:, 0, :], 0, S)
+        scatter(1, 1, h1[:, 1, :], 0, S)
+        scatter(1, 2, h12[:], 0, S)
 
         w3_q = [
             quantize(round_and_interleave(w3_raw[0][:], "w3_bf0", "sq_a3"), "w3_q0"),
             quantize(round_and_interleave(w3_raw[1][:], "w3_bf1", "sq_b3"), "w3_q1"),
         ]
-        x0_q = quantize(round_and_interleave(x0[:], "x0_bf", "sq_a3"), "x0_q")
+        x0_q = quantize(round_and_interleave(x0[:], "x0_bf", "w3_raw1"), "x0_q")
+        h13 = root(late1[3], "h13", "x0")
+        scatter(1, 3, h13[:], 0, S)
 
         NT = N // P
         MQ = M // P
@@ -274,7 +304,7 @@ def tile_list_tyre_wear_wall_kernel(
             stage2_pass(y1[q], y2[q], 0, x0_q[0][:, cols].bitcast(FP8X4), x0_q[1][:, cols])
 
         out_rows = out.rearrange("(t p) m -> p t m", p=P)
-        x1_first = sb([P, 2, PACK, P], F32, "x1_first", "sq_a3")
+        x1_first = sb([P, 2, PACK, P], F32, "x1_first", "x0")
 
         def gather_quarter(q):
             if q < 2:

@@ -22,6 +22,10 @@ P = 128
 PACK = 4
 KP = P * PACK
 LIST = 16
+RUN = 4
+JT = S // P
+NT = N // P
+MQ = M // P
 QUAD_ORDER = (0, 2, 1, 3)
 
 
@@ -41,13 +45,13 @@ def tile_list_tyre_wear_wall_kernel(
         def bank(index, name):
             return psum.tile([P, KP], F32, name=name, tag="bank%d" % index)
 
-        def load_scale_rows(queue, tile, scales):
+        def load_scale_rows(tile, scales):
             for q in QUAD_ORDER:
                 rows = scales[:, 4 * q : 4 * q + 4, :].rearrange("a r c -> r a c")
-                queue.dma_start(out=tile[32 * q : 32 * q + 4, :, :].bitcast(I32), in_=rows.bitcast(I32))
+                nc.sync.dma_start(out=tile[32 * q : 32 * q + 4, :, :].bitcast(I32), in_=rows.bitcast(I32))
 
-        def load_rows(rows, name, tag):
-            raw = sb([P, PACK, rows.shape[1]], F32, name, tag)
+        def load_rows(rows, name):
+            raw = sb([P, PACK, rows.shape[1]], F32, name)
             nc.sync.dma_start(out=raw[:], in_=rows.rearrange("(p i) c -> p i c", i=PACK))
             return raw
 
@@ -55,14 +59,14 @@ def tile_list_tyre_wear_wall_kernel(
             width = planes.shape[2]
             grouped = sb([P, width, PACK], BF16, name, tag)
             copy(
-                out=grouped[:].rearrange("p (c u) i -> p c i u", u=4),
-                in_=planes.rearrange("p i (c u) -> p c i u", u=4),
+                out=grouped[:].rearrange("p (c u) i -> p c i u", u=RUN),
+                in_=planes.rearrange("p i (c u) -> p c i u", u=RUN),
             )
             return grouped
 
-        def quantize(grouped, name, tag=None):
+        def quantize(grouped, name, codes_tag=None):
             width = grouped.shape[1]
-            codes = sb([P, width], U32, name + "_codes", tag)
+            codes = sb([P, width], U32, name + "_codes", codes_tag)
             scales = sb([P, width], U8, name + "_scales")
             nc.vector.quantize_mx(
                 out=codes[:].bitcast(FP8X4), scales=scales[:], in_=grouped[:].rearrange("p c i -> p (c i)")
@@ -89,7 +93,7 @@ def tile_list_tyre_wear_wall_kernel(
 
         def load_w1(b, a, lo, hi):
             name = "w1_raw%d%d_%d" % (b, a, lo)
-            w1_raw[b, a, lo] = load_rows(w1[KP * a : KP * (a + 1), KP * b + lo : KP * b + hi], name, name)
+            w1_raw[b, a, lo] = load_rows(w1[KP * a : KP * (a + 1), KP * b + lo : KP * b + hi], name)
 
         def load_w2(b):
             w2_w[b] = sb([P, 2, 2 * KP], U8, "w2_w%d" % b)
@@ -111,16 +115,16 @@ def tile_list_tyre_wear_wall_kernel(
                     out=wgs_d[pair][32 * q : 32 * (q + 1), :, :], in_=wgs_rows[:, 2 * pair : 2 * pair + 2, :]
                 )
 
-        half = KP // 2
+        piece = KP // 2
         nc.sync.dma_start(idx[:], offs)
-        load_scale_rows(nc.sync, w2_s, w2_scales)
+        load_scale_rows(w2_s, w2_scales)
         load_tab(0)
-        load_scale_rows(nc.sync, tab_s, tab_scales)
+        load_scale_rows(tab_s, tab_scales)
         load_w2(0)
         load_tab(1)
         for a in range(2):
-            load_w1(0, a, 0, half)
-            load_w1(0, a, half, KP)
+            load_w1(0, a, 0, piece)
+            load_w1(0, a, piece, KP)
         nc.sync.dma_start(idx2[:], offs2)
         load_page(0, 0)
         load_wgs(0)
@@ -140,17 +144,18 @@ def tile_list_tyre_wear_wall_kernel(
             load_page(1, i)
         w4_w = sb([P, 2, 2 * N], U8, "w4_w")
         nc.sync.dma_start(out=w4_w[:].bitcast(I32), in_=w4_words.rearrange("a p c -> p a c").bitcast(I32))
-        load_scale_rows(nc.sync, w4_s, w4_scales)
-        mix_t = sb([P, N // P], F32, "mix_t")
+        load_scale_rows(w4_s, w4_scales)
+        mix_t = sb([P, NT], F32, "mix_t")
         with nc.allow_non_contiguous_dma(reason="one value of mix for each partition and output tile"):
             nc.sync.dma_start(out=mix_t[:], in_=mix.rearrange("(t p) -> p t", p=P))
-        w3_raw = [load_rows(w3[KP * a : KP * (a + 1), :], "w3_raw%d" % a, "w3_raw%d" % a) for a in range(2)]
+        w3_raw = [load_rows(w3[KP * a : KP * (a + 1), :], "w3_raw%d" % a) for a in range(2)]
 
         w1_q = {}
 
         def quantize_w1(b, a, lo, tag, copy, codes_tag=None):
             name = "w1_%d%d_%d" % (b, a, lo)
-            codes, scales = quantize(round_and_interleave(w1_raw[b, a, lo][:], name + "_bf", tag, copy), name, codes_tag)
+            grouped = round_and_interleave(w1_raw[b, a, lo][:], name + "_bf", tag, copy)
+            codes, scales = quantize(grouped, name, codes_tag)
             w1_q.setdefault((b, a), []).append((lo, codes, scales))
 
         v_w, v_s = {}, {}
@@ -166,9 +171,7 @@ def tile_list_tyre_wear_wall_kernel(
         gather_words(1)
         for a in range(2):
             quantize_w1(0, a, 0, "bf0", nc.vector.tensor_copy)
-            quantize_w1(0, a, half, "bf1", nc.vector.tensor_copy)
-
-        JT = S // P
+            quantize_w1(0, a, piece, "bf1", nc.vector.tensor_copy)
 
         def stage1(b):
             h = sb([P, 2, S], F32, "h%d" % b)
@@ -183,26 +186,25 @@ def tile_list_tyre_wear_wall_kernel(
             def pass_w1(acc, jt, a):
                 for lo, codes, scales in w1_q[b, a]:
                     hi = lo + codes.shape[1]
-                    mx_pass(acc[:, lo:hi], jt, a, codes[:].bitcast(FP8X4), scales[:], a == 0 and lo == 0, a == 1 and hi == KP)
+                    first, last = a == 0 and lo == 0, a == 1 and hi == KP
+                    mx_pass(acc[:, lo:hi], jt, a, codes[:].bitcast(FP8X4), scales[:], first, last)
 
             def pass_w2(acc, jt, a):
-                mx_pass(acc[:], jt, a, w2_w[b][:, a, :].bitcast(FP4X4), w2_s[:, a, KP * b : KP * (b + 1)], a == 0, a == 1)
+                scales = w2_s[:, a, KP * b : KP * (b + 1)]
+                mx_pass(acc[:], jt, a, w2_w[b][:, a, :].bitcast(FP4X4), scales, a == 0, a == 1)
 
             def square(sq, acc, lo, hi):
                 planes = acc[:].rearrange("p (q i) -> p i q", i=PACK)
                 nc.scalar.activation(sq[:, lo:hi, :], planes[:, lo:hi, :], ACT.Square)
 
             def turn(total, slot, sq, start, stop):
-                nc.tensor.matmul(total[:, P * slot : P * (slot + 1)], sq, ident[:], start=start, stop=stop, is_transpose=True)
-
-            def add_turned(total, slot, jt, i):
-                turn(total, slot, sq_b[jt][:, i, :], True, False)
-                turn(total, slot, sq_a[jt][:, i, :], False, True)
+                cols = slice(P * slot, P * (slot + 1))
+                nc.tensor.matmul(total[:, cols], sq, ident[:], start=start, stop=stop, is_transpose=True)
 
             sq_a, sq_b = {}, {}
             for jt in range(JT):
-                acc_a = bank(jt % 2 if b == 0 else jt, "acc_a%d%d" % (b, jt))
-                acc_b = bank(4 + jt, "acc_b%d%d" % (b, jt))
+                acc_a = bank(jt, "acc_a%d%d" % (b, jt))
+                acc_b = bank(JT + jt, "acc_b%d%d" % (b, jt))
                 sq_a[jt] = sb([P, PACK, P], F32, "sq_a%d%d" % (b, jt), "sq_a%d" % jt)
                 sq_b[jt] = sb([P, PACK, P], F32, "sq_b%d%d" % (b, jt), "sq_b%d" % jt)
                 pass_w2(acc_b, jt, 0)
@@ -211,7 +213,7 @@ def tile_list_tyre_wear_wall_kernel(
                 pass_w1(acc_a, jt, 1)
                 square(sq_b[jt], acc_b, 0, PACK)
                 square(sq_a[jt], acc_a, 0, 2)
-                total = bank(4 + jt, "total%d%d" % (b, jt))
+                total = bank(JT + jt, "total%d%d" % (b, jt))
                 turn(total, 0, sq_b[jt][:, 0, :], True, False)
                 turn(total, 1, sq_b[jt][:, 1, :], False, False)
                 turn(total, 0, sq_a[jt][:, 0, :], False, False)
@@ -225,7 +227,8 @@ def tile_list_tyre_wear_wall_kernel(
             for i in range(2, PACK):
                 late[i] = bank(i, "late%d%d" % (b, i))
                 for jt in range(JT):
-                    add_turned(late[i], jt, jt, i)
+                    turn(late[i], jt, sq_b[jt][:, i, :], True, False)
+                    turn(late[i], jt, sq_a[jt][:, i, :], False, True)
             return h, late
 
         def root(total, name, tag):
@@ -253,9 +256,9 @@ def tile_list_tyre_wear_wall_kernel(
         h0, late0 = stage1(0)
         h02 = root(late0[2], "h02", "h02")
         h03 = root(late0[3], "h03", "h03")
-        for lo, hi in ((0, 128), (128, 256), (256, 384), (384, 512)):
-            scatter(0, 0, h0[:, 0, :], lo, hi)
-            scatter(0, 1, h0[:, 1, :], lo, hi)
+        for jt in range(JT):
+            scatter(0, 0, h0[:, 0, :], P * jt, P * (jt + 1))
+            scatter(0, 1, h0[:, 1, :], P * jt, P * (jt + 1))
         quantize_w1(1, 0, 0, "bf0", nc.scalar.copy)
         scatter(0, 2, h02[:], 0, S)
         quantize_w1(1, 1, 0, "x0", nc.scalar.copy, "h02")
@@ -267,6 +270,7 @@ def tile_list_tyre_wear_wall_kernel(
         x0 = sb([P, PACK, M], F32, "x0", "x0")
         for i in range(PACK):
             gather(x0[:, i, :], 0, i, wg0, 0, M)
+
         scatter(1, 0, h1[:, 0, :], 0, S)
         scatter(1, 1, h1[:, 1, :], 0, S)
         scatter(1, 2, h12[:], 0, S)
@@ -278,9 +282,6 @@ def tile_list_tyre_wear_wall_kernel(
         x0_q = quantize(round_and_interleave(x0[:], "x0_bf", "w3_raw1"), "x0_q")
         h13 = root(late1[3], "h13", "x0")
         scatter(1, 3, h13[:], 0, S)
-
-        NT = N // P
-        MQ = M // P
 
         def stage2_pass(acc1, acc2, a, codes, scales):
             for t in range(NT):
@@ -315,8 +316,8 @@ def tile_list_tyre_wear_wall_kernel(
                 gather(x1[:, i, :], 1, i, wg1, P * q, P * (q + 1))
             return round_and_interleave(x1, "x1_bf%d" % q, "x1_bf%d" % q)
 
-        def multiply_quarter(q, grouped):
-            codes, scales = quantize(grouped, "x1_q%d" % q)
+        def multiply_quarter(q, x1_bf):
+            codes, scales = quantize(x1_bf, "x1_q%d" % q)
             stage2_pass(y1[q], y2[q], 1, codes[:].bitcast(FP8X4), scales[:])
 
         def finish_quarter(q):
@@ -329,11 +330,11 @@ def tile_list_tyre_wear_wall_kernel(
             nc.vector.tensor_tensor(result[:], y2[q][:].rearrange("p (t m) -> p t m", t=NT), mixed[:], ADD)
             nc.sync.dma_start(out=out_rows[:, :, P * q : P * (q + 1)], in_=result[:])
 
-        grouped = {0: gather_quarter(0)}
+        rounded = {0: gather_quarter(0)}
         for q in range(MQ):
             if q + 1 < MQ:
-                grouped[q + 1] = gather_quarter(q + 1)
-            multiply_quarter(q, grouped[q])
+                rounded[q + 1] = gather_quarter(q + 1)
+            multiply_quarter(q, rounded[q])
             if q > 0:
                 finish_quarter(q - 1)
         finish_quarter(MQ - 1)

from contextlib import ExitStack

import concourse.mybir as mybir
from concourse.masks import make_identity

K, T, S, T2, M, H, N = 1024, 2048, 512, 1024, 512, 1024, 512
FLOPS = 2 * (2 * K * H * S + 2 * H * N * M)

F32 = mybir.dt.float32
BF16 = mybir.dt.bfloat16
I32 = mybir.dt.int32
U32 = mybir.dt.uint32
U16 = mybir.dt.uint16
U8 = mybir.dt.uint8
FP8X4 = mybir.dt.float8_e4m3fn_x4
FP4X4 = mybir.dt.float4_e2m1fn_x4
MULT = mybir.AluOpType.mult
ADD = mybir.AluOpType.add
ACT = mybir.ActivationFunctionType

P = 128
PACK = 4
KP = P * PACK
LIST = 16
RUN = 4
JT = S // P
NT = N // P
MQ = M // P
QUAD_ORDER = (0, 2, 1, 3)


def tile_list_tyre_wear_wall_kernel(
    tc, tab_words, tab_scales, offs, w1, w2_words, w2_scales, page0, offs2, wgs, offs3, wgt, gain, w3,
    w4_words, w4_scales, mix, out,
):
    nc = tc.nc
    with ExitStack() as ctx:
        lists = ctx.enter_context(tc.tile_pool(name="lists", bufs=1))
        keep = ctx.enter_context(tc.tile_pool(name="keep", bufs=1))
        psum = ctx.enter_context(tc.psum_pool(name="psum", bufs=1))

        def sb(shape, dtype, name, tag=None):
            return keep.tile(shape, dtype, name=name, tag=tag or name, align_bytes=64)

        def bank(index, name):
            return psum.tile([P, KP], F32, name=name, tag="bank%d" % index)

        def load_scale_rows(tile, scales):
            for q in QUAD_ORDER:
                rows = scales[:, 4 * q : 4 * q + 4, :].rearrange("a r c -> r a c")
                nc.sync.dma_start(out=tile[32 * q : 32 * q + 4, :, :].bitcast(I32), in_=rows.bitcast(I32))

        def load_rows(rows, name):
            raw = sb([P, PACK, rows.shape[1]], F32, name)
            nc.sync.dma_start(out=raw[:], in_=rows.rearrange("(p i) c -> p i c", i=PACK))
            return raw

        def round_and_interleave(planes, name, tag, copy=nc.scalar.copy):
            width = planes.shape[2]
            grouped = sb([P, width, PACK], BF16, name, tag)
            copy(
                out=grouped[:].rearrange("p (c u) i -> p c i u", u=RUN),
                in_=planes.rearrange("p i (c u) -> p c i u", u=RUN),
            )
            return grouped

        def quantize(grouped, name, codes_tag=None):
            width = grouped.shape[1]
            codes = sb([P, width], U32, name + "_codes", codes_tag)
            scales = sb([P, width], U8, name + "_scales")
            nc.vector.quantize_mx(
                out=codes[:].bitcast(FP8X4), scales=scales[:], in_=grouped[:].rearrange("p c i -> p (c i)")
            )
            return codes, scales

        tab_s = sb([P, 2, T], U8, "tab_s")
        nc.vector.memset(tab_s[:].bitcast(I32), 0)
        w2_s = sb([P, 2, H], U8, "w2_s")
        w4_s = sb([P, 2, N], U8, "w4_s")
        one = sb([P, 1], F32, "one")
        nc.gpsimd.memset(one[:], 1.0)
        warm = sb([P, 1], F32, "warm")
        nc.scalar.activation(warm[:], one[:], ACT.Sqrt, bias=one[:])
        ident = sb([P, P], F32, "ident")
        make_identity(nc, ident[:])

        idx = lists.tile([P, S // LIST], U16, name="idx")
        idx2 = lists.tile([P, S // LIST], U16, name="idx2")
        idx3 = lists.tile([P, M // LIST], U16, name="idx3")
        page_rows = page0.rearrange("(b p i) t -> b i p t", b=2, i=PACK)
        wgs_rows = wgs.rearrange("(q i) j -> q i j", i=PACK)
        w1_raw, w2_w, tab_w, pages, wgs_d = {}, {}, {}, {}, {}

        def load_w1(b, a, lo, hi):
            name = "w1_raw%d%d_%d" % (b, a, lo)
            w1_raw[b, a, lo] = load_rows(w1[KP * a : KP * (a + 1), KP * b + lo : KP * b + hi], name)

        def load_w2(b):
            w2_w[b] = sb([P, 2, 2 * KP], U8, "w2_w%d" % b)
            src = w2_words[:, :, 2 * KP * b : 2 * KP * (b + 1)].rearrange("a p c -> p a c")
            nc.sync.dma_start(out=w2_w[b][:].bitcast(I32), in_=src.bitcast(I32))

        def load_tab(a):
            tab_w[a] = sb([P, T], I32, "tab_w%d" % a)
            nc.sync.dma_start(out=tab_w[a][:], in_=tab_words[a].rearrange("p t i -> p (t i)").bitcast(I32))

        def load_page(b, i):
            pages[b, i] = sb([P, T2], F32, "page%d%d" % (b, i))
            nc.sync.dma_start(out=pages[b, i][:], in_=page_rows[b, i])

        def load_wgs(pair):
            wgs_d[pair] = sb([P, 2, S], F32, "wgs%d" % pair)
            for q in QUAD_ORDER:
                nc.sync.dma_start(
                    out=wgs_d[pair][32 * q : 32 * (q + 1), :, :], in_=wgs_rows[:, 2 * pair : 2 * pair + 2, :]
                )

        piece = KP // 2
        nc.sync.dma_start(idx[:], offs)
        load_scale_rows(w2_s, w2_scales)
        load_tab(0)
        load_scale_rows(tab_s, tab_scales)
        load_w2(0)
        load_tab(1)
        for a in range(2):
            load_w1(0, a, 0, piece)
            load_w1(0, a, piece, KP)
        nc.sync.dma_start(idx2[:], offs2)
        load_page(0, 0)
        load_wgs(0)
        load_page(0, 1)
        wgt_t = sb([P, M], F32, "wgt_t")
        nc.sync.dma_start(out=wgt_t[:], in_=wgt)
        gain_t = sb([P, 2, PACK], F32, "gain_t")
        nc.sync.dma_start(out=gain_t[:], in_=gain.rearrange("(b p i) -> p b i", b=2, i=PACK))
        nc.sync.dma_start(idx3[:], offs3)
        load_w1(1, 0, 0, KP)
        load_w1(1, 1, 0, KP)
        load_w2(1)
        load_wgs(1)
        load_page(0, 2)
        load_page(0, 3)
        for i in range(PACK):
            load_page(1, i)
        w4_w = sb([P, 2, 2 * N], U8, "w4_w")
        nc.sync.dma_start(out=w4_w[:].bitcast(I32), in_=w4_words.rearrange("a p c -> p a c").bitcast(I32))
        load_scale_rows(w4_s, w4_scales)
        mix_t = sb([P, NT], F32, "mix_t")
        with nc.allow_non_contiguous_dma(reason="one value of mix for each partition and output tile"):
            nc.sync.dma_start(out=mix_t[:], in_=mix.rearrange("(t p) -> p t", p=P))
        w3_raw = [load_rows(w3[KP * a : KP * (a + 1), :], "w3_raw%d" % a) for a in range(2)]

        w1_q = {}

        def quantize_w1(b, a, lo, tag, copy, codes_tag=None):
            name = "w1_%d%d_%d" % (b, a, lo)
            grouped = round_and_interleave(w1_raw[b, a, lo][:], name + "_bf", tag, copy)
            codes, scales = quantize(grouped, name, codes_tag)
            w1_q.setdefault((b, a), []).append((lo, codes, scales))

        v_w, v_s = {}, {}

        def gather_words(a):
            v_w[a] = sb([P, S], U32, "v_w%d" % a)
            nc.vector.tensor_copy(v_w[a][:], tab_w[a][:].bitcast(U32).indirect(idx[:]))

        gather_words(0)
        for a in range(2):
            v_s[a] = sb([P, S], U8, "v_s%d" % a)
            nc.vector.tensor_copy(v_s[a][:], tab_s[:, a, :].indirect(idx[:]))
        gather_words(1)
        for a in range(2):
            quantize_w1(0, a, 0, "bf0", nc.vector.tensor_copy)
            quantize_w1(0, a, piece, "bf1", nc.vector.tensor_copy)

        def stage1(b):
            h = sb([P, 2, S], F32, "h%d" % b)

            def mx_pass(acc, jt, a, codes, scales, start, stop):
                cols = slice(P * jt, P * (jt + 1))
                nc.tensor.matmul_mx(
                    out=acc, lhsT=v_w[a][:, cols].bitcast(FP8X4), lhsT_scale=v_s[a][:, cols],
                    rhs=codes, rhs_scale=scales, start=start, stop=stop,
                )

            def pass_w1(acc, jt, a):
                for lo, codes, scales in w1_q[b, a]:
                    hi = lo + codes.shape[1]
                    first, last = a == 0 and lo == 0, a == 1 and hi == KP
                    mx_pass(acc[:, lo:hi], jt, a, codes[:].bitcast(FP8X4), scales[:], first, last)

            def pass_w2(acc, jt, a):
                scales = w2_s[:, a, KP * b : KP * (b + 1)]
                mx_pass(acc[:], jt, a, w2_w[b][:, a, :].bitcast(FP4X4), scales, a == 0, a == 1)

            def square(sq, acc, lo, hi):
                planes = acc[:].rearrange("p (q i) -> p i q", i=PACK)
                nc.scalar.activation(sq[:, lo:hi, :], planes[:, lo:hi, :], ACT.Square)

            def turn(total, slot, sq, start, stop):
                cols = slice(P * slot, P * (slot + 1))
                nc.tensor.matmul(total[:, cols], sq, ident[:], start=start, stop=stop, is_transpose=True)

            sq_a, sq_b = {}, {}
            for jt in range(JT):
                acc_a = bank(jt, "acc_a%d%d" % (b, jt))
                acc_b = bank(JT + jt, "acc_b%d%d" % (b, jt))
                sq_a[jt] = sb([P, PACK, P], F32, "sq_a%d%d" % (b, jt), "sq_a%d" % jt)
                sq_b[jt] = sb([P, PACK, P], F32, "sq_b%d%d" % (b, jt), "sq_b%d" % jt)
                pass_w2(acc_b, jt, 0)
                pass_w1(acc_a, jt, 0)
                pass_w2(acc_b, jt, 1)
                pass_w1(acc_a, jt, 1)
                square(sq_b[jt], acc_b, 0, PACK)
                square(sq_a[jt], acc_a, 0, 2)
                total = bank(JT + jt, "total%d%d" % (b, jt))
                turn(total, 0, sq_b[jt][:, 0, :], True, False)
                turn(total, 1, sq_b[jt][:, 1, :], False, False)
                turn(total, 0, sq_a[jt][:, 0, :], False, False)
                turn(total, 1, sq_a[jt][:, 1, :], False, True)
                nc.scalar.activation(
                    h[:, :, P * jt : P * (jt + 1)], total[:, 0 : 2 * P].rearrange("p (i j) -> p i j", i=2),
                    ACT.Sqrt, bias=one[:],
                )
                square(sq_a[jt], acc_a, 2, PACK)
            late = {}
            for i in range(2, PACK):
                late[i] = bank(i, "late%d%d" % (b, i))
                for jt in range(JT):
                    turn(late[i], jt, sq_b[jt][:, i, :], True, False)
                    turn(late[i], jt, sq_a[jt][:, i, :], False, True)
            return h, late

        def root(total, name, tag):
            h = sb([P, S], F32, name, tag)
            nc.scalar.activation(h[:], total[:], ACT.Sqrt, bias=one[:])
            return h

        def scatter(b, i, h, lo, hi):
            nc.vector.tensor_tensor(
                pages[b, i][:].indirect(idx2[:, lo // LIST : hi // LIST]),
                h[:, lo:hi], wgs_d[i // 2][:, i % 2, lo:hi], MULT,
            )

        def weights(b):
            wg = sb([P, PACK, M], F32, "wg%d" % b)
            for i in range(PACK):
                nc.scalar.activation(wg[:, i, :], wgt_t[:], ACT.Copy, scale=gain_t[:, b, i : i + 1])
            return wg

        def gather(dst, b, i, wg, lo, hi):
            nc.vector.tensor_tensor(
                dst, pages[b, i][:].indirect(idx3[:, lo // LIST : hi // LIST]), wg[:, i, lo:hi], MULT
            )

        h0, late0 = stage1(0)
        h02 = root(late0[2], "h02", "h02")
        h03 = root(late0[3], "h03", "h03")
        for jt in range(JT):
            scatter(0, 0, h0[:, 0, :], P * jt, P * (jt + 1))
            scatter(0, 1, h0[:, 1, :], P * jt, P * (jt + 1))
        quantize_w1(1, 0, 0, "bf0", nc.scalar.copy)
        scatter(0, 2, h02[:], 0, S)
        quantize_w1(1, 1, 0, "x0", nc.scalar.copy, "h02")
        wg0 = weights(0)
        scatter(0, 3, h03[:], 0, S)
        h1, late1 = stage1(1)
        h12 = root(late1[2], "h12", "h12")
        wg1 = weights(1)
        x0 = sb([P, PACK, M], F32, "x0", "x0")
        for i in range(PACK):
            gather(x0[:, i, :], 0, i, wg0, 0, M)

        scatter(1, 0, h1[:, 0, :], 0, S)
        scatter(1, 1, h1[:, 1, :], 0, S)
        scatter(1, 2, h12[:], 0, S)

        w3_q = [
            quantize(round_and_interleave(w3_raw[0][:], "w3_bf0", "sq_a3"), "w3_q0"),
            quantize(round_and_interleave(w3_raw[1][:], "w3_bf1", "sq_b3"), "w3_q1"),
        ]
        x0_q = quantize(round_and_interleave(x0[:], "x0_bf", "w3_raw1"), "x0_q")
        h13 = root(late1[3], "h13", "x0")
        scatter(1, 3, h13[:], 0, S)

        def stage2_pass(acc1, acc2, a, codes, scales):
            for t in range(NT):
                cols = slice(P * t, P * (t + 1))
                nc.tensor.matmul_mx(
                    out=acc1[:, cols], lhsT=w3_q[a][0][:, cols].bitcast(FP8X4), lhsT_scale=w3_q[a][1][:, cols],
                    rhs=codes, rhs_scale=scales, start=(a == 0 and t == 0), stop=(a == 1 and t == NT - 1),
                )
            for t in range(NT):
                cols = slice(P * t, P * (t + 1))
                nc.tensor.matmul_mx(
                    out=acc2[:, cols], lhsT=w4_w[:, a, 2 * P * t : 2 * P * (t + 1)].bitcast(FP4X4),
                    lhsT_scale=w4_s[:, a, cols],
                    rhs=codes, rhs_scale=scales, start=(a == 0 and t == 0), stop=(a == 1 and t == NT - 1),
                )

        y1 = [bank(2 * q, "y1_%d" % q) for q in range(MQ)]
        y2 = [bank(2 * q + 1, "y2_%d" % q) for q in range(MQ)]
        for q in range(MQ):
            cols = slice(P * q, P * (q + 1))
            stage2_pass(y1[q], y2[q], 0, x0_q[0][:, cols].bitcast(FP8X4), x0_q[1][:, cols])

        out_rows = out.rearrange("(t p) m -> p t m", p=P)
        x1_first = sb([P, 2, PACK, P], F32, "x1_first", "x0")

        def gather_quarter(q):
            if q < 2:
                x1 = x1_first[:, q, :, :]
            else:
                x1 = sb([P, PACK, P], F32, "x1_%d" % q, "x1_bf%d" % (q - 2))[:]
            for i in range(PACK):
                gather(x1[:, i, :], 1, i, wg1, P * q, P * (q + 1))
            return round_and_interleave(x1, "x1_bf%d" % q, "x1_bf%d" % q)

        def multiply_quarter(q, x1_bf):
            codes, scales = quantize(x1_bf, "x1_q%d" % q)
            stage2_pass(y1[q], y2[q], 1, codes[:].bitcast(FP8X4), scales[:])

        def finish_quarter(q):
            mixed = sb([P, NT, P], F32, "mixed%d" % q)
            for t in range(NT):
                nc.scalar.activation(
                    mixed[:, t, :], y1[q][:, P * t : P * (t + 1)], ACT.Copy, scale=mix_t[:, t : t + 1]
                )
            result = sb([P, NT, P], F32, "result%d" % q)
            nc.vector.tensor_tensor(result[:], y2[q][:].rearrange("p (t m) -> p t m", t=NT), mixed[:], ADD)
            nc.sync.dma_start(out=out_rows[:, :, P * q : P * (q + 1)], in_=result[:])

        rounded = {0: gather_quarter(0)}
        for q in range(MQ):
            if q + 1 < MQ:
                rounded[q + 1] = gather_quarter(q + 1)
            multiply_quarter(q, rounded[q])
            if q > 0:
                finish_quarter(q - 1)
        finish_quarter(MQ - 1)
